import numpy as np
import ml_dtypes


def mxq(x, axis, fmt="e4m3"):
    dtype, down = {"e4m3": (ml_dtypes.float8_e4m3fn, 7), "e5m2": (ml_dtypes.float8_e5m2, 14)}[fmt]
    v = np.moveaxis(np.asarray(x, np.float32).astype(ml_dtypes.bfloat16).astype(np.float64), axis, -1)
    blocks = v.reshape(v.shape[:-1] + (-1, 32))
    amax = np.abs(blocks).max(-1, keepdims=True)
    byte = np.maximum(np.where(amax > 0, np.frexp(amax)[1] - 1 + 127, 0) - down, 1)
    scale = np.exp2(byte - 127.0)
    codes = (blocks / scale).astype(np.float32).astype(dtype).astype(np.float64)
    return np.moveaxis((codes * scale).reshape(v.shape), -1, axis)


WIDE = False


def mx_kscale(k):
    if not WIDE:
        return np.ones(k)
    levels = np.array([10, -10, 5, -5, 0])
    if k % 512:
        return np.exp2(np.random.permutation(np.resize(levels, k // 32))).repeat(32)
    a = np.empty((k // 512, 16))
    for p in range(k // 512):
        a[p, :8] = np.random.permutation(np.resize(levels, 8))
        for g in range(8):
            far = levels[np.abs(levels - a[p, g]) >= 10]
            a[p, g + 8] = far[np.random.randint(len(far))]
    return np.exp2(a.ravel()).repeat(32)


def f64(x):
    return np.asarray(x).astype(np.float64)


def striped(idx):
    return np.tile(idx.reshape(-1, 16).T, (8, 1)).astype(np.uint16)


def unstriped(offs):
    return offs[:16].T.reshape(-1).astype(np.int64)


def striped8(idx):
    return np.concatenate([x.reshape(-1, 16).T for x in idx]).astype(np.uint16)


def runs(offs, k):
    lists = np.stack([offs[16 * r : 16 * r + 16].T.reshape(-1) for r in range(8)]).astype(np.int64)
    return lists[np.arange(k) % 512 // 64]


def pack_weight(w):
    k, n = w.shape
    w = f64(np.asarray(w, np.float32).astype(ml_dtypes.bfloat16)).reshape(k // 32, 32, n)
    amax = np.abs(w).max(1)
    byte = np.clip(np.where(amax > 0, np.frexp(amax)[1] - 1 + 127 - 7, 1), 1, 254)
    scaled = (w * np.exp2(127.0 - byte)[:, None, :]).reshape(k, n).astype(np.float32)
    words = np.ascontiguousarray(scaled.reshape(k // 512, 128, 4, n).transpose(0, 1, 3, 2)).astype(ml_dtypes.float8_e4m3fn).view(np.uint8)
    return words, np.ascontiguousarray(byte.astype(np.uint8).reshape(k // 512, 16, n))


def unpack_weight(words, scales):
    g, p, n, _ = words.shape
    vals = np.ascontiguousarray(words).view(ml_dtypes.float8_e4m3fn).astype(np.float64) * np.repeat(np.exp2(scales.astype(np.float64) - 127.0), 8, axis=1)[..., None]
    return vals.transpose(0, 1, 3, 2).reshape(g * 512, n)

def planes(y):
    n, m = y.shape
    v = y.astype(np.float32).astype(ml_dtypes.bfloat16).astype(np.float64).reshape(n // 32, 32, m)
    top = np.abs(v).max(1)
    byte = np.clip(np.where(top > 0, np.frexp(top)[1] - 1 + 127 - 7, 1), 1, 254)
    codes = (v * np.exp2(127.0 - byte)[:, None, :]).reshape(n, m).astype(np.float32).astype(ml_dtypes.float8_e4m3fn).view(np.uint8)
    words = codes.reshape(n // 512, 128, 4, m).transpose(0, 1, 3, 2)
    return np.ascontiguousarray(words), np.ascontiguousarray(byte.astype(np.uint8).reshape(n // 512, 16, m))


K, T, S, V, N, H = 512, 2048, 512, 256, 512, 512


def setup_inputs():
    n = np.random.standard_normal
    s = mx_kscale(K)[:, None]
    u = mx_kscale(H)
    packed_xT = pack_weight(n((K, T)) * s)
    packed_w3 = pack_weight(n((H, N)) / np.sqrt(H) / u[:, None])
    perm = np.stack([np.random.permutation(S) for _ in range(8)])
    return {
        "x_words": packed_xT[0],
        "x_scales": packed_xT[1],
        "w1": (n((K, H)) / np.sqrt(K) / s * u).astype(np.float32),
        "w2": (n((H, H)) / np.sqrt(H) / u[:, None] * u).astype(np.float32),
        "res": (2 * n((N, S))).astype(np.float32),
        "w3_words": packed_w3[0],
        "w3_scales": packed_w3[1],
        "offs": striped(np.random.permutation(T)[:S]),
        "la": striped8(perm[:, :V]),
        "lb": striped8(perm[:, V:]),
        "mate": striped8(np.stack([np.random.permutation(S) for _ in range(8)])),
    }


def reference(x_words, x_scales, w1, w2, res, w3_words, w3_scales, offs, la, lb, mate):
    xq = unpack_weight(x_words, x_scales)[:, unstriped(offs)]
    y = mxq(f64(w1), 0, "e4m3").T @ xq
    a = y[np.arange(H)[:, None], runs(la, H)]
    b = y[np.arange(H)[:, None], runs(lb, H)]
    mx = np.maximum(a, b)
    mn = np.minimum(a, b)
    p = np.zeros((H, S))
    p[np.arange(H)[:, None], runs(la, H)] = mn
    z = p.copy()
    z[np.arange(H)[:, None], runs(lb, H)] = mx
    h = mxq(f64(w2), 0, "e4m3").T @ mxq(z, 0, "e4m3")
    z2 = np.maximum(h, h[np.arange(H)[:, None], runs(mate, H)])
    out_0 = f64(res) + (unpack_weight(w3_words, w3_scales).T @ mxq(z2, 0, "e4m3"))
    return (out_0,) + planes(out_0)

@@ -1,0 +1,275 @@
+from contextlib import ExitStack
+
+import concourse.mybir as mybir
+
+K, T, S, V, N, H = 512, 2048, 512, 256, 512, 512
+FLOPS = 2 * (K * H * S + H * H * S + H * N * S)
+
+F32 = mybir.dt.float32
+BF16 = mybir.dt.bfloat16
+I32 = mybir.dt.int32
+U32 = mybir.dt.uint32
+U16 = mybir.dt.uint16
+U8 = mybir.dt.uint8
+FP8X4 = mybir.dt.float8_e4m3fn_x4
+ALU = mybir.AluOpType
+ACT = mybir.ActivationFunctionType
+
+P = 128
+PACK = 4
+HALF = S // 2
+LIST_COLS = HALF // 16
+
+
+def tile_picked_sortlay_none_po_kernel(
+    tc, x_words, x_scales, w1, w2, res, w3_words, w3_scales, offs, la, lb, mate, out_0, out_1, out_2
+):
+    nc = tc.nc
+    with ExitStack() as ctx:
+        sb = ctx.enter_context(tc.tile_pool(name="sb", bufs=1))
+        psum = ctx.enter_context(tc.psum_pool(name="psum", bufs=1))
+
+        def tile(name, shape, dtype, tag=None):
+            return sb.tile(shape, dtype, name=name, tag=tag or name, align_bytes=64)
+
+        def bank(name, number, shape):
+            return psum.tile(shape, F32, name=name, tag="bank%d" % number)
+
+        def half(h):
+            return slice(h * HALF, (h + 1) * HALF)
+
+        def load_scale_rows(queue, plane, rows):
+            for q in range(4):
+                queue.dma_start(out=plane[32 * q : 32 * q + 4, :].bitcast(I32), in_=rows[0, 4 * q : 4 * q + 4, :].bitcast(I32))
+
+        def deal_weight(copy, dealt, raw, h):
+            copy(
+                out=dealt[:, :, 64 * h : 64 * (h + 1), :].rearrange("p t m j -> p m j t"),
+                in_=raw[:].rearrange("p j (m t) -> p m j t", t=PACK),
+            )
+
+        def interleave(copy, out, planar):
+            copy(
+                out=out.rearrange("p (c i) t -> p c t i", i=4),
+                in_=planar.rearrange("p t (c i) -> p c t i", i=4),
+            )
+
+        def quantize(codes, scales, values):
+            nc.vector.quantize_mx(out=codes.bitcast(FP8X4), scales=scales, in_=values)
+
+        def column_tiles(codes, scales, count):
+            return [(codes[:, t * P : (t + 1) * P], scales[:, t * P : (t + 1) * P]) for t in range(count)]
+
+        def multiply(out, weight, codes, scales):
+            nc.tensor.matmul_mx(
+                out=out,
+                lhsT=weight[0].bitcast(FP8X4),
+                lhsT_scale=weight[1],
+                rhs=codes.bitcast(FP8X4),
+                rhs_scale=scales,
+                start=True,
+                stop=True,
+            )
+
+        offs_sb = sb.tile([P, S // 16], U16, name="offs_sb")
+        la_sb = sb.tile([P, V // 16], U16, name="la_sb")
+        lb_sb = sb.tile([P, V // 16], U16, name="lb_sb")
+        mate_sb = sb.tile([P, S // 16], U16, name="mate_sb")
+        w1_raw = [tile("w1_raw%d" % h, [P, PACK, HALF], F32) for h in range(2)]
+        x_words_sb = tile("x_words_sb", [P, T], U32)
+        x_scales_sb = tile("x_scales_sb", [P, T], U8)
+
+        nc.vector.memset(x_scales_sb[:].bitcast(I32), 0)
+        load_scale_rows(nc.scalar, x_scales_sb, x_scales)
+        nc.sync.dma_start(offs_sb[:], offs)
+        nc.sync.dma_start(la_sb[:], la)
+        nc.sync.dma_start(lb_sb[:], lb)
+        for h in range(2):
+            nc.sync.dma_start(out=w1_raw[h][:], in_=w1[:, half(h)].rearrange("(p j) c -> p j c", j=PACK))
+        nc.sync.dma_start(out=x_words_sb[:].bitcast(I32), in_=x_words[0].rearrange("p n t -> p (n t)").bitcast(I32))
+        nc.sync.dma_start(mate_sb[:], mate)
+
+        w1_dealt = tile("w1_dealt", [P, PACK, P, PACK], BF16)
+        deal_weight(nc.scalar.copy, w1_dealt, w1_raw[0], 0)
+        deal_weight(nc.vector.tensor_copy, w1_dealt, w1_raw[1], 1)
+        w1_codes = tile("w1_codes", [P, H], U32)
+        w1_scales = tile("w1_scales", [P, H], U8)
+        quantize(w1_codes[:], w1_scales[:], w1_dealt[:].rearrange("p t m j -> p (t m j)"))
+
+        picked_scales = tile("picked_scales", [P, S], U8)
+        nc.vector.tensor_copy(picked_scales[:], x_scales_sb[:].indirect(offs_sb[:]))
+        picked_words = tile("picked_words", [P, S], U32)
+        halves = ((0, HALF), (HALF, S))
+        for lo, hi in halves:
+            nc.vector.tensor_copy(picked_words[:, lo:hi], x_words_sb[:].indirect(offs_sb[:, lo // 16 : hi // 16]))
+
+        w3_words_sb = tile("w3_words_sb", [P, N], I32, tag="w1_raw0")
+        nc.sync.dma_start(out=w3_words_sb[:], in_=w3_words[0].rearrange("p n t -> p (n t)").bitcast(I32))
+        w2_raw = [tile("w2_raw%d" % h, [P, PACK, HALF], F32, tag=("w1_raw1", "w1_dealt")[h]) for h in range(2)]
+        for h in range(2):
+            nc.sync.dma_start(out=w2_raw[h][:], in_=w2[:, half(h)].rearrange("(p j) c -> p j c", j=PACK))
+        w3_scales_sb = tile("w3_scales_sb", [P, N], U8, tag="x_scales_sb")
+        nc.gpsimd.memset(w3_scales_sb[:].bitcast(I32), 0)
+        load_scale_rows(nc.sync, w3_scales_sb, w3_scales)
+        res_sb = tile("res_sb", [P, PACK, S], F32, tag="x_words_sb")
+        nc.sync.dma_start(out=res_sb[:], in_=res.rearrange("(p t) c -> p t c", t=PACK))
+
+        def product_rows(name, order, pieces, banks, weights, codes, scales, split_second):
+            rows = {t: tile("%s%d" % (name, t), [P, S], F32) for t in order}
+            first = order[0]
+            for (lo, hi), number in zip(pieces, banks):
+                acc = bank("%s_first%d" % (name, lo), number, [P, hi - lo])
+                multiply(acc[:], weights[first], codes[:, lo:hi], scales[:, lo:hi])
+                nc.scalar.copy(out=rows[first][:, lo:hi], in_=acc[:])
+            for t, number in zip(order[1:], banks[len(pieces) :]):
+                acc = bank("%s_acc%d" % (name, t), number, [P, S])
+                for lo, hi in pieces if split_second and t == order[1] else ((0, S),):
+                    multiply(acc[:, lo:hi], weights[t], codes[:, lo:hi], scales[:, lo:hi])
+                nc.scalar.copy(out=rows[t][:], in_=acc[:])
+            return rows
+
+        order = (2, 0, 1, 3)
+        y = product_rows("y", order, halves, (0, 1, 2, 3, 4), column_tiles(w1_codes, w1_scales, PACK), picked_words, picked_scales, False)
+
+        w3_codes = tile("w3_codes", [P, N], I32)
+        nc.vector.tensor_copy(
+            out=w3_codes[:].rearrange("p (t m) -> p m t", t=PACK), in_=w3_words_sb[:].rearrange("p (m t) -> p m t", t=PACK)
+        )
+
+        a = tile("a", [P, PACK, V], F32)
+        steps = [tile("steps%d" % u, [P, 2, 2, V], F32) for u in range(2)]
+        for u in range(2):
+            diff = tile("sorted_bf%d" % u, [P, 2, V], F32)
+            for i in range(2):
+                nc.vector.tensor_copy(a[:, 2 * u + i, :], y[order[2 * u + i]][:].indirect(la_sb[:]))
+            for i in range(2):
+                nc.vector.tensor_tensor(diff[:, i, :], y[order[2 * u + i]][:].indirect(lb_sb[:]), a[:, 2 * u + i, :], ALU.subtract)
+            drop = tile("drop%d" % u, [P, 2, V], F32)
+            nc.scalar.activation(steps[u][:, 0], diff[:], ACT.Relu)
+            nc.scalar.activation(drop[:], diff[:], ACT.Relu, scale=-1.0)
+            nc.scalar.activation(steps[u][:, 1], drop[:], ACT.Copy, scale=-1.0)
+
+        w2_dealt = tile("w2_dealt", [P, PACK, P, PACK], BF16, tag="sorted_bf0")
+        for h in range(2):
+            deal_weight(nc.scalar.copy, w2_dealt, w2_raw[h], h)
+        w2_first_codes = tile("w2_first_codes", [P, 2 * P], U32)
+        w2_first_scales = tile("w2_first_scales", [P, 2 * P], U8)
+        quantize(w2_first_codes[:], w2_first_scales[:], w2_dealt[:, :2].rearrange("p t m j -> p (t m j)"))
+
+        z = {t: sb.tile([P, S], F32, name="z%d" % t) for t in order}
+        z_bf = [tile("z_bf%d" % h, [P, HALF, PACK], BF16) for h in range(2)]
+        for u in range(2):
+            for s, places in enumerate((lb_sb, la_sb)):
+                for i in range(2):
+                    t = order[2 * u + i]
+                    nc.vector.tensor_tensor(z[t][:].indirect(places[:]), a[:, 2 * u + i, :], steps[u][:, s, i, :], ALU.add)
+                    if s == 1 and t == order[0]:
+                        both = z[t][:, half(0)].unsqueeze(2).to_broadcast([P, HALF, 2])
+                        nc.scalar.copy(out=z_bf[0][:, :, t : t + 2], in_=both)
+                        nc.scalar.copy(out=z_bf[1][:, :, t], in_=z[t][:, half(1)])
+                    elif s == 1 and t != order[-1]:
+                        for h in range(2):
+                            nc.scalar.copy(out=z_bf[h][:, :, t], in_=z[t][:, half(h)])
+        last = order[-1]
+        nc.vector.tensor_copy(out=z_bf[0][:, :, last], in_=z[last][:, half(0)])
+        nc.scalar.copy(out=z_bf[1][:, :, last], in_=z[last][:, half(1)])
+        z_codes = tile("z_codes", [P, S], U32)
+        z_scales = tile("z_scales", [P, S], U8)
+        for h in range(2):
+            quantize(z_codes[:, half(h)], z_scales[:, half(h)], z_bf[h][:].rearrange("p c t -> p (c t)"))
+        w2_rest_codes = tile("w2_rest_codes", [P, 2 * P], U32, tag="z_bf1")
+        w2_rest_scales = tile("w2_rest_scales", [P, 2 * P], U8)
+        quantize(w2_rest_codes[:], w2_rest_scales[:], w2_dealt[:, 2:].rearrange("p t m j -> p (t m j)"))
+
+        w2_tiles = column_tiles(w2_first_codes, w2_first_scales, 2) + column_tiles(w2_rest_codes, w2_rest_scales, 2)
+        hid = product_rows("h", range(PACK), halves, (5, 6, 7, 0, 1), w2_tiles, z_codes, z_scales, True)
+
+        w3_dealt_scales = tile("w3_dealt_scales", [P, N], U8, tag="sorted_bf0")
+        nc.vector.tensor_copy(
+            out=w3_dealt_scales[:].rearrange("p (t m) -> p m t", t=PACK),
+            in_=w3_scales_sb[:].rearrange("p (m t) -> p m t", t=PACK),
+        )
+
+        w3_tiles = column_tiles(w3_codes, w3_dealt_scales, PACK)
+        UNIT = 128
+        spans = ((0, 256), (256, 384), (384, 512))
+        stage = tile("stage", [P, 12 * UNIT], BF16)
+
+        def staged(slot, c):
+            width = spans[c][1] - spans[c][0]
+            return stage[:, slot * UNIT : slot * UNIT + PACK * width]
+
+        fetched = [staged(slot, c).rearrange("p (t c) -> p t c", t=PACK) for c, slot in enumerate((2, 0, 2))]
+        z2_bf = [staged(4, 0), tile("z2_bf1", [P, PACK * UNIT], BF16), tile("z2_bf2", [P, PACK * UNIT], BF16)]
+        z2_codes = tile("z2_codes", [P, S], U32)
+        z2_scales = [tile("z2_scales%d" % c, [P, hi - lo], U8) for c, (lo, hi) in enumerate(spans)]
+        out_codes = tile("out_codes", [P, S], U32)
+        out_scales = tile("out_scales", [P, S], U8)
+        out_rows = out_0.rearrange("(p t) c -> p t c", t=PACK)
+        out_words = out_1[0].rearrange("p n t -> p (n t)").bitcast(I32)
+        result_bf = [tile("result_bf%d" % h, [P, HALF, PACK], BF16) for h in range(2)]
+
+        def fetch(c, planes):
+            lo, hi = spans[c]
+            for t in planes:
+                nc.vector.tensor_copy(fetched[c][:, t, :], hid[t][:].indirect(mate_sb[:, lo // 16 : hi // 16]))
+
+        def compete(c, tag=None):
+            lo, hi = spans[c]
+            h_bf = tile("h_bf%d" % c, [P, PACK, hi - lo], BF16)
+            for t in range(PACK):
+                nc.scalar.copy(out=h_bf[:, t, :], in_=hid[t][:, lo:hi])
+            z2 = tile("z2_%d" % c, [P, PACK, hi - lo], BF16, tag=tag)
+            nc.vector.tensor_tensor(z2[:], fetched[c], h_bf[:], ALU.max)
+            interleave(nc.scalar.copy, z2_bf[c][:].rearrange("p (c t) -> p c t", t=PACK), z2[:])
+
+        def third_product(c):
+            lo, hi = spans[c]
+            quantize(z2_codes[:, lo:hi], z2_scales[c][:], z2_bf[c][:])
+            accs = []
+            for start in range(lo, hi, UNIT):
+                acc = bank("out_acc%d" % start, 2 + start // UNIT, [P, PACK, UNIT])
+                for t in range(PACK):
+                    cols = slice(start - lo, start - lo + UNIT)
+                    multiply(acc[:, t, :], w3_tiles[t], z2_codes[:, start : start + UNIT], z2_scales[c][:, cols])
+                accs.append(acc)
+            return accs
+
+        def add_residual(c, accs, tag=None):
+            lo, hi = spans[c]
+            result = tile("result%d" % c, [P, PACK, hi - lo], F32, tag=tag)
+            for i, acc in enumerate(accs):
+                start = lo + i * UNIT
+                part = result[:, :, i * UNIT : (i + 1) * UNIT]
+                nc.vector.tensor_tensor(part, acc[:], res_sb[:, :, start : start + UNIT], ALU.add)
+                rounded = result_bf[start // HALF][:, start % HALF : start % HALF + UNIT, :]
+                if c < 2:
+                    interleave(nc.scalar.copy, rounded, part)
+                else:
+                    interleave(nc.scalar.copy, rounded[:, :48, :], part[:, :, :48])
+                    interleave(nc.vector.tensor_copy, rounded[:, 48:, :], part[:, :, 48:])
+            nc.sync.dma_start(out=out_rows[:, :, lo:hi], in_=result[:])
+
+        def hand_on(h):
+            quantize(out_codes[:, half(h)], out_scales[:, half(h)], result_bf[h][:].rearrange("p c t -> p (c t)"))
+            nc.sync.dma_start(out=out_words[:, half(h)], in_=out_codes[:, half(h)].bitcast(I32))
+
+        fetch(0, range(PACK))
+        fetch(1, (0, 1))
+        compete(0)
+        fetch(1, (2, 3))
+        compete(1)
+        fetch(2, (0, 1))
+        accs0 = third_product(0)
+        fetch(2, (2, 3))
+        accs1 = third_product(1)
+        compete(2, tag="z2_bf1")
+        add_residual(0, accs0, tag="h_bf2")
+        accs2 = third_product(2)
+        add_residual(1, accs1)
+        hand_on(0)
+        add_residual(2, accs2)
+        hand_on(1)
+        for q in range(4):
+            queue = nc.sync if q % 2 else nc.scalar
+            queue.dma_start(out=out_2[0, 4 * q : 4 * q + 4, :].bitcast(I32), in_=out_scales[32 * q : 32 * q + 4, :].bitcast(I32))

@@ -75,23 +75,27 @@ def tile_picked_sortlay_none_po_kernel(
         la_sb = sb.tile([P, V // 16], U16, name="la_sb")
         lb_sb = sb.tile([P, V // 16], U16, name="lb_sb")
         mate_sb = sb.tile([P, S // 16], U16, name="mate_sb")
-        w1_raw = [tile("w1_raw%d" % h, [P, PACK, HALF], F32) for h in range(2)]
+        w1_raw = [tile("w1_raw%d" % u, [P, 2, H], F32) for u in range(2)]
         x_words_sb = tile("x_words_sb", [P, T], U32)
         x_scales_sb = tile("x_scales_sb", [P, T], U8)
 
         nc.vector.memset(x_scales_sb[:].bitcast(I32), 0)
         load_scale_rows(nc.scalar, x_scales_sb, x_scales)
+        w1_rows = w1.rearrange("(p j) c -> p j c", j=PACK)
         nc.sync.dma_start(offs_sb[:], offs)
         nc.sync.dma_start(la_sb[:], la)
         nc.sync.dma_start(lb_sb[:], lb)
-        for h in range(2):
-            nc.sync.dma_start(out=w1_raw[h][:], in_=w1[:, half(h)].rearrange("(p j) c -> p j c", j=PACK))
+        nc.sync.dma_start(out=w1_raw[0][:], in_=w1_rows[:, :2, :])
+        nc.sync.dma_start(out=w1_raw[1][:], in_=w1_rows[:, 2:, :])
         nc.sync.dma_start(out=x_words_sb[:].bitcast(I32), in_=x_words[0].rearrange("p n t -> p (n t)").bitcast(I32))
         nc.sync.dma_start(mate_sb[:], mate)
 
         w1_dealt = tile("w1_dealt", [P, PACK, P, PACK], BF16)
-        deal_weight(nc.scalar.copy, w1_dealt, w1_raw[0], 0)
-        deal_weight(nc.vector.tensor_copy, w1_dealt, w1_raw[1], 1)
+        for u, copy in enumerate((nc.scalar.copy, nc.vector.tensor_copy)):
+            copy(
+                out=w1_dealt[:, :, :, 2 * u : 2 * u + 2].rearrange("p t m j -> p m j t"),
+                in_=w1_raw[u][:].rearrange("p j (m t) -> p m j t", t=PACK),
+            )
         w1_codes = tile("w1_codes", [P, H], U32)
         w1_scales = tile("w1_scales", [P, H], U8)
         quantize(w1_codes[:], w1_scales[:], w1_dealt[:].rearrange("p t m j -> p (t m j)"))
@@ -193,14 +197,14 @@ def tile_picked_sortlay_none_po_kernel(
         w3_tiles = column_tiles(w3_codes, w3_dealt_scales, PACK)
         UNIT = 128
         spans = ((0, 256), (256, 384), (384, 512))
-        stage = tile("stage", [P, 12 * UNIT], BF16)
+        stage = tile("stage", [P, 13 * UNIT], BF16)
 
         def staged(slot, c):
             width = spans[c][1] - spans[c][0]
             return stage[:, slot * UNIT : slot * UNIT + PACK * width]
 
         fetched = [staged(slot, c).rearrange("p (t c) -> p t c", t=PACK) for c, slot in enumerate((2, 0, 2))]
-        z2_bf = [staged(4, 0), tile("z2_bf1", [P, PACK * UNIT], BF16), tile("z2_bf2", [P, PACK * UNIT], BF16)]
+        z2_bf = [staged(5, 0), tile("z2_bf1", [P, PACK * UNIT], BF16), tile("z2_bf2", [P, PACK * UNIT], BF16)]
         z2_codes = tile("z2_codes", [P, S], U32)
         z2_scales = [tile("z2_scales%d" % c, [P, hi - lo], U8) for c, (lo, hi) in enumerate(spans)]
         out_codes = tile("out_codes", [P, S], U32)
@@ -216,11 +220,8 @@ def tile_picked_sortlay_none_po_kernel(
 
         def compete(c, tag=None):
             lo, hi = spans[c]
-            h_bf = tile("h_bf%d" % c, [P, PACK, hi - lo], BF16)
-            for t in range(PACK):
-                nc.scalar.copy(out=h_bf[:, t, :], in_=hid[t][:, lo:hi])
             z2 = tile("z2_%d" % c, [P, PACK, hi - lo], BF16, tag=tag)
-            nc.vector.tensor_tensor(z2[:], fetched[c], h_bf[:], ALU.max)
+            nc.vector.tensor_tensor(z2[:], fetched[c], h_bf[lo // HALF][:, :, lo % HALF : lo % HALF + hi - lo], ALU.max)
             interleave(nc.scalar.copy, z2_bf[c][:].rearrange("p (c t) -> p c t", t=PACK), z2[:])
 
         def third_product(c):
@@ -235,40 +236,47 @@ def tile_picked_sortlay_none_po_kernel(
                 accs.append(acc)
             return accs
 
-        def add_residual(c, accs, tag=None):
+        results = [tile("result%d" % c, [P, PACK, hi - lo], F32) for c, (lo, hi) in enumerate(spans)]
+
+        def add_residual(c, i, acc):
             lo, hi = spans[c]
-            result = tile("result%d" % c, [P, PACK, hi - lo], F32, tag=tag)
-            for i, acc in enumerate(accs):
-                start = lo + i * UNIT
-                part = result[:, :, i * UNIT : (i + 1) * UNIT]
-                nc.vector.tensor_tensor(part, acc[:], res_sb[:, :, start : start + UNIT], ALU.add)
-                rounded = result_bf[start // HALF][:, start % HALF : start % HALF + UNIT, :]
-                if c < 2:
-                    interleave(nc.scalar.copy, rounded, part)
-                else:
-                    interleave(nc.scalar.copy, rounded[:, :48, :], part[:, :, :48])
-                    interleave(nc.vector.tensor_copy, rounded[:, 48:, :], part[:, :, 48:])
-            nc.sync.dma_start(out=out_rows[:, :, lo:hi], in_=result[:])
+            start = lo + i * UNIT
+            part = results[c][:, :, i * UNIT : (i + 1) * UNIT]
+            nc.vector.tensor_tensor(part, acc[:], res_sb[:, :, start : start + UNIT], ALU.add)
+            rounded = result_bf[start // HALF][:, start % HALF : start % HALF + UNIT, :]
+            if c < 2:
+                interleave(nc.scalar.copy, rounded, part)
+            else:
+                interleave(nc.scalar.copy, rounded[:, :48, :], part[:, :, :48])
+                interleave(nc.vector.tensor_copy, rounded[:, 48:, :], part[:, :, 48:])
+            if start + UNIT == hi:
+                nc.sync.dma_start(out=out_rows[:, :, lo:hi], in_=results[c][:])
 
         def hand_on(h):
             quantize(out_codes[:, half(h)], out_scales[:, half(h)], result_bf[h][:].rearrange("p c t -> p (c t)"))
             nc.sync.dma_start(out=out_words[:, half(h)], in_=out_codes[:, half(h)].bitcast(I32))
 
+        h_bf = [tile("h_bf%d" % h, [P, PACK, HALF], BF16) for h in range(2)]
+        for h in range(2):
+            for t in range(PACK):
+                nc.scalar.copy(out=h_bf[h][:, t, :], in_=hid[t][:, half(h)])
         fetch(0, range(PACK))
         fetch(1, (0, 1))
         compete(0)
         fetch(1, (2, 3))
+        fetch(2, (2,))
         compete(1)
         fetch(2, (0, 1))
         accs0 = third_product(0)
-        fetch(2, (2, 3))
+        fetch(2, (3,))
         accs1 = third_product(1)
-        compete(2, tag="z2_bf1")
-        add_residual(0, accs0, tag="h_bf2")
+        compete(2)
+        add_residual(0, 0, accs0[0])
+        add_residual(0, 1, accs0[1])
         accs2 = third_product(2)
-        add_residual(1, accs1)
+        add_residual(1, 0, accs1[0])
         hand_on(0)
-        add_residual(2, accs2)
+        add_residual(2, 0, accs2[0])
         hand_on(1)
         for q in range(4):
             queue = nc.sync if q % 2 else nc.scalar

@@ -16,9 +16,14 @@ ALU = mybir.AluOpType
 ACT = mybir.ActivationFunctionType
 
 P = 128
-PACK = 4
+PLANES = 4
+PER_COLUMN = 16
 HALF = S // 2
-LIST_COLS = HALF // 16
+HALVES = ((0, HALF), (HALF, S))
+SORT_ORDER = (0, 2, 3, 1)
+UNIT = 128
+SPANS = ((0, 2 * UNIT), (2 * UNIT, 3 * UNIT), (3 * UNIT, 4 * UNIT))
+SCALAR_ROUNDS = 48
 
 
 def tile_picked_sortlay_none_po_kernel(
@@ -38,15 +43,17 @@ def tile_picked_sortlay_none_po_kernel(
         def half(h):
             return slice(h * HALF, (h + 1) * HALF)
 
+        def entries(offsets, lo, hi):
+            return offsets[:, lo // PER_COLUMN : hi // PER_COLUMN]
+
+        def as_words(packed):
+            return packed[0].rearrange("p n t -> p (n t)").bitcast(I32)
+
         def load_scale_rows(queue, plane, rows):
             for q in range(4):
-                queue.dma_start(out=plane[32 * q : 32 * q + 4, :].bitcast(I32), in_=rows[0, 4 * q : 4 * q + 4, :].bitcast(I32))
-
-        def deal_weight(copy, dealt, raw, h):
-            copy(
-                out=dealt[:, :, 64 * h : 64 * (h + 1), :].rearrange("p t m j -> p m j t"),
-                in_=raw[:].rearrange("p j (m t) -> p m j t", t=PACK),
-            )
+                queue.dma_start(
+                    out=plane[32 * q : 32 * q + 4, :].bitcast(I32), in_=rows[0, 4 * q : 4 * q + 4, :].bitcast(I32)
+                )
 
         def interleave(copy, out, planar):
             copy(
@@ -57,210 +64,221 @@ def tile_picked_sortlay_none_po_kernel(
         def quantize(codes, scales, values):
             nc.vector.quantize_mx(out=codes.bitcast(FP8X4), scales=scales, in_=values)
 
-        def column_tiles(codes, scales, count):
-            return [(codes[:, t * P : (t + 1) * P], scales[:, t * P : (t + 1) * P]) for t in range(count)]
+        def stationary_tiles(codes, scales, count):
+            return [(codes[:, i * P : (i + 1) * P], scales[:, i * P : (i + 1) * P]) for i in range(count)]
 
-        def multiply(out, weight, codes, scales):
+        def multiply(out, stationary, codes, scales):
             nc.tensor.matmul_mx(
                 out=out,
-                lhsT=weight[0].bitcast(FP8X4),
-                lhsT_scale=weight[1],
+                lhsT=stationary[0].bitcast(FP8X4),
+                lhsT_scale=stationary[1],
                 rhs=codes.bitcast(FP8X4),
                 rhs_scale=scales,
                 start=True,
                 stop=True,
             )
 
-        offs_sb = sb.tile([P, S // 16], U16, name="offs_sb")
-        la_sb = sb.tile([P, V // 16], U16, name="la_sb")
-        lb_sb = sb.tile([P, V // 16], U16, name="lb_sb")
-        mate_sb = sb.tile([P, S // 16], U16, name="mate_sb")
+        def product_planes(name, order, banks, weights, codes, scales, second_by_halves):
+            planes = {t: tile("%s%d" % (name, t), [P, S], F32) for t in order}
+            for (lo, hi), number in zip(HALVES, banks):
+                acc = bank("%s_first%d" % (name, lo), number, [P, hi - lo])
+                multiply(acc[:], weights[order[0]], codes[:, lo:hi], scales[:, lo:hi])
+                nc.scalar.copy(out=planes[order[0]][:, lo:hi], in_=acc[:])
+            for t, number in zip(order[1:], banks[len(HALVES) :]):
+                acc = bank("%s_acc%d" % (name, t), number, [P, S])
+                for lo, hi in HALVES if second_by_halves and t == order[1] else ((0, S),):
+                    multiply(acc[:, lo:hi], weights[t], codes[:, lo:hi], scales[:, lo:hi])
+                nc.scalar.copy(out=planes[t][:], in_=acc[:])
+            return planes
+
+        offs_sb = sb.tile([P, S // PER_COLUMN], U16, name="offs_sb")
+        la_sb = sb.tile([P, V // PER_COLUMN], U16, name="la_sb")
+        lb_sb = sb.tile([P, V // PER_COLUMN], U16, name="lb_sb")
+        mate_sb = sb.tile([P, S // PER_COLUMN], U16, name="mate_sb")
         w1_raw = [tile("w1_raw%d" % u, [P, 2, H], F32) for u in range(2)]
         x_words_sb = tile("x_words_sb", [P, T], U32)
         x_scales_sb = tile("x_scales_sb", [P, T], U8)
 
         nc.vector.memset(x_scales_sb[:].bitcast(I32), 0)
         load_scale_rows(nc.scalar, x_scales_sb, x_scales)
-        w1_rows = w1.rearrange("(p j) c -> p j c", j=PACK)
+        w1_rows = w1.rearrange("(p j) c -> p j c", j=PLANES)
         nc.sync.dma_start(offs_sb[:], offs)
         nc.sync.dma_start(la_sb[:], la)
         nc.sync.dma_start(lb_sb[:], lb)
         nc.sync.dma_start(out=w1_raw[0][:], in_=w1_rows[:, :2, :])
         nc.sync.dma_start(out=w1_raw[1][:], in_=w1_rows[:, 2:, :])
-        nc.sync.dma_start(out=x_words_sb[:].bitcast(I32), in_=x_words[0].rearrange("p n t -> p (n t)").bitcast(I32))
+        nc.sync.dma_start(out=x_words_sb[:].bitcast(I32), in_=as_words(x_words))
         nc.sync.dma_start(mate_sb[:], mate)
 
-        w1_dealt = tile("w1_dealt", [P, PACK, P, PACK], BF16)
+        w1_dealt = tile("w1_dealt", [P, PLANES, P, PLANES], BF16)
         for u, copy in enumerate((nc.scalar.copy, nc.vector.tensor_copy)):
             copy(
                 out=w1_dealt[:, :, :, 2 * u : 2 * u + 2].rearrange("p t m j -> p m j t"),
-                in_=w1_raw[u][:].rearrange("p j (m t) -> p m j t", t=PACK),
+                in_=w1_raw[u][:].rearrange("p j (m t) -> p m j t", t=PLANES),
             )
-        w1_codes = tile("w1_codes", [P, H], U32)
-        w1_scales = tile("w1_scales", [P, H], U8)
-        quantize(w1_codes[:], w1_scales[:], w1_dealt[:].rearrange("p t m j -> p (t m j)"))
+        w1_first_codes = tile("w1_first_codes", [P, P], U32)
+        w1_first_scales = tile("w1_first_scales", [P, P], U8)
+        quantize(w1_first_codes[:], w1_first_scales[:], w1_dealt[:, 0].rearrange("p m j -> p (m j)"))
 
         picked_scales = tile("picked_scales", [P, S], U8)
         nc.vector.tensor_copy(picked_scales[:], x_scales_sb[:].indirect(offs_sb[:]))
         picked_words = tile("picked_words", [P, S], U32)
-        halves = ((0, HALF), (HALF, S))
-        for lo, hi in halves:
-            nc.vector.tensor_copy(picked_words[:, lo:hi], x_words_sb[:].indirect(offs_sb[:, lo // 16 : hi // 16]))
+        for lo, hi in HALVES:
+            nc.vector.tensor_copy(picked_words[:, lo:hi], x_words_sb[:].indirect(entries(offs_sb, lo, hi)))
+
+        w1_rest_codes = tile("w1_rest_codes", [P, 3 * P], U32, tag="x_words_sb")
+        w1_rest_scales = tile("w1_rest_scales", [P, 3 * P], U8)
+        quantize(w1_rest_codes[:, P:], w1_rest_scales[:, P:], w1_dealt[:, 2:].rearrange("p t m j -> p (t m j)"))
+        quantize(w1_rest_codes[:, :P], w1_rest_scales[:, :P], w1_dealt[:, 1].rearrange("p m j -> p (m j)"))
+        w1_tiles = stationary_tiles(w1_first_codes, w1_first_scales, 1) + stationary_tiles(w1_rest_codes, w1_rest_scales, 3)
 
         w3_words_sb = tile("w3_words_sb", [P, N], I32, tag="w1_raw0")
-        nc.sync.dma_start(out=w3_words_sb[:], in_=w3_words[0].rearrange("p n t -> p (n t)").bitcast(I32))
-        w2_raw = [tile("w2_raw%d" % h, [P, PACK, HALF], F32, tag=("w1_raw1", "w1_dealt")[h]) for h in range(2)]
+        nc.sync.dma_start(out=w3_words_sb[:], in_=as_words(w3_words))
+        w2_raw = [tile("w2_raw%d" % h, [P, PLANES, H // 2], F32, tag=tag) for h, tag in enumerate(("w1_raw1", "w1_dealt"))]
         for h in range(2):
-            nc.sync.dma_start(out=w2_raw[h][:], in_=w2[:, half(h)].rearrange("(p j) c -> p j c", j=PACK))
+            nc.sync.dma_start(out=w2_raw[h][:], in_=w2[:, half(h)].rearrange("(p j) c -> p j c", j=PLANES))
         w3_scales_sb = tile("w3_scales_sb", [P, N], U8, tag="x_scales_sb")
         nc.gpsimd.memset(w3_scales_sb[:].bitcast(I32), 0)
         load_scale_rows(nc.sync, w3_scales_sb, w3_scales)
-        res_sb = tile("res_sb", [P, PACK, S], F32, tag="x_words_sb")
-        nc.sync.dma_start(out=res_sb[:], in_=res.rearrange("(p t) c -> p t c", t=PACK))
 
-        def product_rows(name, order, pieces, banks, weights, codes, scales, split_second):
-            rows = {t: tile("%s%d" % (name, t), [P, S], F32) for t in order}
-            first = order[0]
-            for (lo, hi), number in zip(pieces, banks):
-                acc = bank("%s_first%d" % (name, lo), number, [P, hi - lo])
-                multiply(acc[:], weights[first], codes[:, lo:hi], scales[:, lo:hi])
-                nc.scalar.copy(out=rows[first][:, lo:hi], in_=acc[:])
-            for t, number in zip(order[1:], banks[len(pieces) :]):
-                acc = bank("%s_acc%d" % (name, t), number, [P, S])
-                for lo, hi in pieces if split_second and t == order[1] else ((0, S),):
-                    multiply(acc[:, lo:hi], weights[t], codes[:, lo:hi], scales[:, lo:hi])
-                nc.scalar.copy(out=rows[t][:], in_=acc[:])
-            return rows
-
-        order = (2, 0, 1, 3)
-        y = product_rows("y", order, halves, (0, 1, 2, 3, 4), column_tiles(w1_codes, w1_scales, PACK), picked_words, picked_scales, False)
+        y = product_planes("y", SORT_ORDER, (0, 1, 2, 3, 4), w1_tiles, picked_words, picked_scales, False)
 
         w3_codes = tile("w3_codes", [P, N], I32)
         nc.vector.tensor_copy(
-            out=w3_codes[:].rearrange("p (t m) -> p m t", t=PACK), in_=w3_words_sb[:].rearrange("p (m t) -> p m t", t=PACK)
+            out=w3_codes[:].rearrange("p (t m) -> p m t", t=PLANES),
+            in_=w3_words_sb[:].rearrange("p (m t) -> p m t", t=PLANES),
         )
 
-        a = tile("a", [P, PACK, V], F32)
+        res_sb = tile("res_sb", [P, PLANES, S], F32, tag="x_words_sb")
+        nc.sync.dma_start(out=res_sb[:], in_=res.rearrange("(p t) c -> p t c", t=PLANES))
+
+        a = tile("a", [P, PLANES, V], F32)
         steps = [tile("steps%d" % u, [P, 2, 2, V], F32) for u in range(2)]
         for u in range(2):
-            diff = tile("sorted_bf%d" % u, [P, 2, V], F32)
+            diff = tile("diff%d" % u, [P, 2, V], F32)
             for i in range(2):
-                nc.vector.tensor_copy(a[:, 2 * u + i, :], y[order[2 * u + i]][:].indirect(la_sb[:]))
+                nc.vector.tensor_copy(a[:, 2 * u + i, :], y[SORT_ORDER[2 * u + i]][:].indirect(la_sb[:]))
             for i in range(2):
-                nc.vector.tensor_tensor(diff[:, i, :], y[order[2 * u + i]][:].indirect(lb_sb[:]), a[:, 2 * u + i, :], ALU.subtract)
+                looked_up = y[SORT_ORDER[2 * u + i]][:].indirect(lb_sb[:])
+                nc.vector.tensor_tensor(diff[:, i, :], looked_up, a[:, 2 * u + i, :], ALU.subtract)
             drop = tile("drop%d" % u, [P, 2, V], F32)
             nc.scalar.activation(steps[u][:, 0], diff[:], ACT.Relu)
             nc.scalar.activation(drop[:], diff[:], ACT.Relu, scale=-1.0)
             nc.scalar.activation(steps[u][:, 1], drop[:], ACT.Copy, scale=-1.0)
 
-        w2_dealt = tile("w2_dealt", [P, PACK, P, PACK], BF16, tag="sorted_bf0")
+        w2_dealt = tile("w2_dealt", [P, PLANES, P, PLANES], BF16, tag="diff0")
         for h in range(2):
-            deal_weight(nc.scalar.copy, w2_dealt, w2_raw[h], h)
+            nc.scalar.copy(
+                out=w2_dealt[:, :, h * P // 2 : (h + 1) * P // 2, :].rearrange("p t m j -> p m j t"),
+                in_=w2_raw[h][:].rearrange("p j (m t) -> p m j t", t=PLANES),
+            )
         w2_first_codes = tile("w2_first_codes", [P, 2 * P], U32)
         w2_first_scales = tile("w2_first_scales", [P, 2 * P], U8)
         quantize(w2_first_codes[:], w2_first_scales[:], w2_dealt[:, :2].rearrange("p t m j -> p (t m j)"))
 
-        z = {t: sb.tile([P, S], F32, name="z%d" % t) for t in order}
-        z_bf = [tile("z_bf%d" % h, [P, HALF, PACK], BF16) for h in range(2)]
+        z = {t: sb.tile([P, S], F32, name="z%d" % t) for t in SORT_ORDER}
+        z_bf = [tile("z_bf%d" % h, [P, HALF, PLANES], BF16) for h in range(2)]
+        first, last = SORT_ORDER[0], SORT_ORDER[-1]
         for u in range(2):
             for s, places in enumerate((lb_sb, la_sb)):
                 for i in range(2):
-                    t = order[2 * u + i]
+                    t = SORT_ORDER[2 * u + i]
                     nc.vector.tensor_tensor(z[t][:].indirect(places[:]), a[:, 2 * u + i, :], steps[u][:, s, i, :], ALU.add)
-                    if s == 1 and t == order[0]:
-                        both = z[t][:, half(0)].unsqueeze(2).to_broadcast([P, HALF, 2])
-                        nc.scalar.copy(out=z_bf[0][:, :, t : t + 2], in_=both)
-                        nc.scalar.copy(out=z_bf[1][:, :, t], in_=z[t][:, half(1)])
-                    elif s == 1 and t != order[-1]:
+                    finished = s == 1
+                    if finished and t == first:
+                        for h in range(2):
+                            twice = z[t][:, half(h)].unsqueeze(2).to_broadcast([P, HALF, 2])
+                            nc.scalar.copy(out=z_bf[h][:, :, t : t + 2], in_=twice)
+                    elif finished and t != last:
                         for h in range(2):
                             nc.scalar.copy(out=z_bf[h][:, :, t], in_=z[t][:, half(h)])
-        last = order[-1]
+        quarter = S // 4
         nc.vector.tensor_copy(out=z_bf[0][:, :, last], in_=z[last][:, half(0)])
-        nc.scalar.copy(out=z_bf[1][:, :, last], in_=z[last][:, half(1)])
+        nc.vector.tensor_copy(out=z_bf[1][:, :quarter, last], in_=z[last][:, HALF : HALF + quarter])
+        nc.scalar.copy(out=z_bf[1][:, quarter:, last], in_=z[last][:, HALF + quarter :])
         z_codes = tile("z_codes", [P, S], U32)
         z_scales = tile("z_scales", [P, S], U8)
         for h in range(2):
             quantize(z_codes[:, half(h)], z_scales[:, half(h)], z_bf[h][:].rearrange("p c t -> p (c t)"))
+
         w2_rest_codes = tile("w2_rest_codes", [P, 2 * P], U32, tag="z_bf1")
         w2_rest_scales = tile("w2_rest_scales", [P, 2 * P], U8)
         quantize(w2_rest_codes[:], w2_rest_scales[:], w2_dealt[:, 2:].rearrange("p t m j -> p (t m j)"))
+        w2_tiles = stationary_tiles(w2_first_codes, w2_first_scales, 2) + stationary_tiles(w2_rest_codes, w2_rest_scales, 2)
+        hidden = product_planes("h", range(PLANES), (5, 6, 7, 0, 1), w2_tiles, z_codes, z_scales, True)
 
-        w2_tiles = column_tiles(w2_first_codes, w2_first_scales, 2) + column_tiles(w2_rest_codes, w2_rest_scales, 2)
-        hid = product_rows("h", range(PACK), halves, (5, 6, 7, 0, 1), w2_tiles, z_codes, z_scales, True)
-
-        w3_dealt_scales = tile("w3_dealt_scales", [P, N], U8, tag="sorted_bf0")
+        w3_dealt_scales = tile("w3_dealt_scales", [P, N], U8, tag="diff0")
         nc.vector.tensor_copy(
-            out=w3_dealt_scales[:].rearrange("p (t m) -> p m t", t=PACK),
-            in_=w3_scales_sb[:].rearrange("p (m t) -> p m t", t=PACK),
+            out=w3_dealt_scales[:].rearrange("p (t m) -> p m t", t=PLANES),
+            in_=w3_scales_sb[:].rearrange("p (m t) -> p m t", t=PLANES),
         )
+        w3_tiles = stationary_tiles(w3_codes, w3_dealt_scales, PLANES)
 
-        w3_tiles = column_tiles(w3_codes, w3_dealt_scales, PACK)
-        UNIT = 128
-        spans = ((0, 256), (256, 384), (384, 512))
         stage = tile("stage", [P, 13 * UNIT], BF16)
 
         def staged(slot, c):
-            width = spans[c][1] - spans[c][0]
-            return stage[:, slot * UNIT : slot * UNIT + PACK * width]
+            lo, hi = SPANS[c]
+            return stage[:, slot * UNIT : slot * UNIT + PLANES * (hi - lo)]
 
-        fetched = [staged(slot, c).rearrange("p (t c) -> p t c", t=PACK) for c, slot in enumerate((2, 0, 2))]
-        z2_bf = [staged(5, 0), tile("z2_bf1", [P, PACK * UNIT], BF16), tile("z2_bf2", [P, PACK * UNIT], BF16)]
+        fetched = [staged(slot, c).rearrange("p (t c) -> p t c", t=PLANES) for c, slot in enumerate((2, 0, 2))]
+        z2_bf = [staged(5, 0), tile("z2_bf1", [P, PLANES * UNIT], BF16), tile("z2_bf2", [P, PLANES * UNIT], BF16)]
         z2_codes = tile("z2_codes", [P, S], U32)
-        z2_scales = [tile("z2_scales%d" % c, [P, hi - lo], U8) for c, (lo, hi) in enumerate(spans)]
+        z2_scales = [tile("z2_scales%d" % c, [P, hi - lo], U8) for c, (lo, hi) in enumerate(SPANS)]
         out_codes = tile("out_codes", [P, S], U32)
         out_scales = tile("out_scales", [P, S], U8)
-        out_rows = out_0.rearrange("(p t) c -> p t c", t=PACK)
-        out_words = out_1[0].rearrange("p n t -> p (n t)").bitcast(I32)
-        result_bf = [tile("result_bf%d" % h, [P, HALF, PACK], BF16) for h in range(2)]
+        out_rows = out_0.rearrange("(p t) c -> p t c", t=PLANES)
+        out_words = as_words(out_1)
+        result_bf = [tile("result_bf%d" % h, [P, HALF, PLANES], BF16) for h in range(2)]
+        results = [tile("result%d" % c, [P, PLANES, hi - lo], F32) for c, (lo, hi) in enumerate(SPANS)]
+        hidden_bf = [tile("hidden_bf%d" % h, [P, PLANES, HALF], BF16) for h in range(2)]
 
         def fetch(c, planes):
-            lo, hi = spans[c]
+            lo, hi = SPANS[c]
             for t in planes:
-                nc.vector.tensor_copy(fetched[c][:, t, :], hid[t][:].indirect(mate_sb[:, lo // 16 : hi // 16]))
+                nc.vector.tensor_copy(fetched[c][:, t, :], hidden[t][:].indirect(entries(mate_sb, lo, hi)))
 
-        def compete(c, tag=None):
-            lo, hi = spans[c]
-            z2 = tile("z2_%d" % c, [P, PACK, hi - lo], BF16, tag=tag)
-            nc.vector.tensor_tensor(z2[:], fetched[c], h_bf[lo // HALF][:, :, lo % HALF : lo % HALF + hi - lo], ALU.max)
-            interleave(nc.scalar.copy, z2_bf[c][:].rearrange("p (c t) -> p c t", t=PACK), z2[:])
+        def compete(c):
+            lo, hi = SPANS[c]
+            own = hidden_bf[lo // HALF][:, :, lo % HALF : lo % HALF + hi - lo]
+            z2 = tile("z2_%d" % c, [P, PLANES, hi - lo], BF16)
+            nc.vector.tensor_tensor(z2[:], fetched[c], own, ALU.max)
+            interleave(nc.scalar.copy, z2_bf[c][:].rearrange("p (c t) -> p c t", t=PLANES), z2[:])
 
         def third_product(c):
-            lo, hi = spans[c]
+            lo, hi = SPANS[c]
             quantize(z2_codes[:, lo:hi], z2_scales[c][:], z2_bf[c][:])
             accs = []
             for start in range(lo, hi, UNIT):
-                acc = bank("out_acc%d" % start, 2 + start // UNIT, [P, PACK, UNIT])
-                for t in range(PACK):
-                    cols = slice(start - lo, start - lo + UNIT)
-                    multiply(acc[:, t, :], w3_tiles[t], z2_codes[:, start : start + UNIT], z2_scales[c][:, cols])
+                acc = bank("out_acc%d" % start, 2 + start // UNIT, [P, PLANES, UNIT])
+                codes = z2_codes[:, start : start + UNIT]
+                scales = z2_scales[c][:, start - lo : start - lo + UNIT]
+                for t in range(PLANES):
+                    multiply(acc[:, t, :], w3_tiles[t], codes, scales)
                 accs.append(acc)
             return accs
 
-        results = [tile("result%d" % c, [P, PACK, hi - lo], F32) for c, (lo, hi) in enumerate(spans)]
-
-        def add_residual(c, i, acc):
-            lo, hi = spans[c]
-            start = lo + i * UNIT
-            part = results[c][:, :, i * UNIT : (i + 1) * UNIT]
-            nc.vector.tensor_tensor(part, acc[:], res_sb[:, :, start : start + UNIT], ALU.add)
-            rounded = result_bf[start // HALF][:, start % HALF : start % HALF + UNIT, :]
-            if c < 2:
-                interleave(nc.scalar.copy, rounded, part)
-            else:
-                interleave(nc.scalar.copy, rounded[:, :48, :], part[:, :, :48])
-                interleave(nc.vector.tensor_copy, rounded[:, 48:, :], part[:, :, 48:])
-            if start + UNIT == hi:
-                nc.sync.dma_start(out=out_rows[:, :, lo:hi], in_=results[c][:])
+        def add_residual(c, accs):
+            lo, hi = SPANS[c]
+            for i, acc in enumerate(accs):
+                start = lo + i * UNIT
+                part = results[c][:, :, i * UNIT : (i + 1) * UNIT]
+                nc.vector.tensor_tensor(part, acc[:], res_sb[:, :, start : start + UNIT], ALU.add)
+                rounded = result_bf[start // HALF][:, start % HALF : start % HALF + UNIT, :]
+                if c < len(SPANS) - 1:
+                    interleave(nc.scalar.copy, rounded, part)
+                else:
+                    interleave(nc.scalar.copy, rounded[:, :SCALAR_ROUNDS, :], part[:, :, :SCALAR_ROUNDS])
+                    interleave(nc.vector.tensor_copy, rounded[:, SCALAR_ROUNDS:, :], part[:, :, SCALAR_ROUNDS:])
+            nc.sync.dma_start(out=out_rows[:, :, lo:hi], in_=results[c][:])
 
         def hand_on(h):
             quantize(out_codes[:, half(h)], out_scales[:, half(h)], result_bf[h][:].rearrange("p c t -> p (c t)"))
             nc.sync.dma_start(out=out_words[:, half(h)], in_=out_codes[:, half(h)].bitcast(I32))
 
-        h_bf = [tile("h_bf%d" % h, [P, PACK, HALF], BF16) for h in range(2)]
         for h in range(2):
-            for t in range(PACK):
-                nc.scalar.copy(out=h_bf[h][:, t, :], in_=hid[t][:, half(h)])
-        fetch(0, range(PACK))
+            for t in range(PLANES):
+                nc.scalar.copy(out=hidden_bf[h][:, t, :], in_=hidden[t][:, half(h)])
+        fetch(0, range(PLANES))
         fetch(1, (0, 1))
         compete(0)
         fetch(1, (2, 3))
@@ -271,13 +289,14 @@ def tile_picked_sortlay_none_po_kernel(
         fetch(2, (3,))
         accs1 = third_product(1)
         compete(2)
-        add_residual(0, 0, accs0[0])
-        add_residual(0, 1, accs0[1])
+        add_residual(0, accs0)
         accs2 = third_product(2)
-        add_residual(1, 0, accs1[0])
+        add_residual(1, accs1)
         hand_on(0)
-        add_residual(2, 0, accs2[0])
+        add_residual(2, accs2)
         hand_on(1)
         for q in range(4):
             queue = nc.sync if q % 2 else nc.scalar
-            queue.dma_start(out=out_2[0, 4 * q : 4 * q + 4, :].bitcast(I32), in_=out_scales[32 * q : 32 * q + 4, :].bitcast(I32))
+            queue.dma_start(
+                out=out_2[0, 4 * q : 4 * q + 4, :].bitcast(I32), in_=out_scales[32 * q : 32 * q + 4, :].bitcast(I32)
+            )

from contextlib import ExitStack

import concourse.mybir as mybir

K, T, S, V, N, H = 512, 2048, 512, 256, 512, 512
FLOPS = 2 * (K * H * S + H * H * S + H * N * S)

F32 = mybir.dt.float32
BF16 = mybir.dt.bfloat16
I32 = mybir.dt.int32
U32 = mybir.dt.uint32
U16 = mybir.dt.uint16
U8 = mybir.dt.uint8
FP8X4 = mybir.dt.float8_e4m3fn_x4
ALU = mybir.AluOpType
ACT = mybir.ActivationFunctionType

P = 128
PLANES = 4
PER_COLUMN = 16
HALF = S // 2
HALVES = ((0, HALF), (HALF, S))
SORT_ORDER = (0, 2, 3, 1)
UNIT = 128
SPANS = ((0, 2 * UNIT), (2 * UNIT, 3 * UNIT), (3 * UNIT, 4 * UNIT))
SCALAR_ROUNDS = 48


def tile_picked_sortlay_none_po_kernel(
    tc, x_words, x_scales, w1, w2, res, w3_words, w3_scales, offs, la, lb, mate, out_0, out_1, out_2
):
    nc = tc.nc
    with ExitStack() as ctx:
        sb = ctx.enter_context(tc.tile_pool(name="sb", bufs=1))
        psum = ctx.enter_context(tc.psum_pool(name="psum", bufs=1))

        def tile(name, shape, dtype, tag=None):
            return sb.tile(shape, dtype, name=name, tag=tag or name, align_bytes=64)

        def bank(name, number, shape):
            return psum.tile(shape, F32, name=name, tag="bank%d" % number)

        def half(h):
            return slice(h * HALF, (h + 1) * HALF)

        def entries(offsets, lo, hi):
            return offsets[:, lo // PER_COLUMN : hi // PER_COLUMN]

        def as_words(packed):
            return packed[0].rearrange("p n t -> p (n t)").bitcast(I32)

        def load_scale_rows(queue, plane, rows):
            for q in range(4):
                queue.dma_start(
                    out=plane[32 * q : 32 * q + 4, :].bitcast(I32), in_=rows[0, 4 * q : 4 * q + 4, :].bitcast(I32)
                )

        def interleave(copy, out, planar):
            copy(
                out=out.rearrange("p (c i) t -> p c t i", i=4),
                in_=planar.rearrange("p t (c i) -> p c t i", i=4),
            )

        def quantize(codes, scales, values):
            nc.vector.quantize_mx(out=codes.bitcast(FP8X4), scales=scales, in_=values)

        def stationary_tiles(codes, scales, count):
            return [(codes[:, i * P : (i + 1) * P], scales[:, i * P : (i + 1) * P]) for i in range(count)]

        def multiply(out, stationary, codes, scales):
            nc.tensor.matmul_mx(
                out=out,
                lhsT=stationary[0].bitcast(FP8X4),
                lhsT_scale=stationary[1],
                rhs=codes.bitcast(FP8X4),
                rhs_scale=scales,
                start=True,
                stop=True,
            )

        def product_planes(name, order, banks, weights, codes, scales, second_by_halves):
            planes = {t: tile("%s%d" % (name, t), [P, S], F32) for t in order}
            for (lo, hi), number in zip(HALVES, banks):
                acc = bank("%s_first%d" % (name, lo), number, [P, hi - lo])
                multiply(acc[:], weights[order[0]], codes[:, lo:hi], scales[:, lo:hi])
                nc.scalar.copy(out=planes[order[0]][:, lo:hi], in_=acc[:])
            for t, number in zip(order[1:], banks[len(HALVES) :]):
                acc = bank("%s_acc%d" % (name, t), number, [P, S])
                for lo, hi in HALVES if second_by_halves and t == order[1] else ((0, S),):
                    multiply(acc[:, lo:hi], weights[t], codes[:, lo:hi], scales[:, lo:hi])
                nc.scalar.copy(out=planes[t][:], in_=acc[:])
            return planes

        offs_sb = sb.tile([P, S // PER_COLUMN], U16, name="offs_sb")
        la_sb = sb.tile([P, V // PER_COLUMN], U16, name="la_sb")
        lb_sb = sb.tile([P, V // PER_COLUMN], U16, name="lb_sb")
        mate_sb = sb.tile([P, S // PER_COLUMN], U16, name="mate_sb")
        w1_raw = [tile("w1_raw%d" % u, [P, 2, H], F32) for u in range(2)]
        x_words_sb = tile("x_words_sb", [P, T], U32)
        x_scales_sb = tile("x_scales_sb", [P, T], U8)

        nc.vector.memset(x_scales_sb[:].bitcast(I32), 0)
        load_scale_rows(nc.scalar, x_scales_sb, x_scales)
        w1_rows = w1.rearrange("(p j) c -> p j c", j=PLANES)
        nc.sync.dma_start(offs_sb[:], offs)
        nc.sync.dma_start(la_sb[:], la)
        nc.sync.dma_start(lb_sb[:], lb)
        nc.sync.dma_start(out=w1_raw[0][:], in_=w1_rows[:, :2, :])
        nc.sync.dma_start(out=w1_raw[1][:], in_=w1_rows[:, 2:, :])
        nc.sync.dma_start(out=x_words_sb[:].bitcast(I32), in_=as_words(x_words))
        nc.sync.dma_start(mate_sb[:], mate)

        w1_dealt = tile("w1_dealt", [P, PLANES, P, PLANES], BF16)
        for u, copy in enumerate((nc.scalar.copy, nc.vector.tensor_copy)):
            copy(
                out=w1_dealt[:, :, :, 2 * u : 2 * u + 2].rearrange("p t m j -> p m j t"),
                in_=w1_raw[u][:].rearrange("p j (m t) -> p m j t", t=PLANES),
            )
        w1_first_codes = tile("w1_first_codes", [P, P], U32)
        w1_first_scales = tile("w1_first_scales", [P, P], U8)
        quantize(w1_first_codes[:], w1_first_scales[:], w1_dealt[:, 0].rearrange("p m j -> p (m j)"))

        picked_scales = tile("picked_scales", [P, S], U8)
        nc.vector.tensor_copy(picked_scales[:], x_scales_sb[:].indirect(offs_sb[:]))
        picked_words = tile("picked_words", [P, S], U32)
        for lo, hi in HALVES:
            nc.vector.tensor_copy(picked_words[:, lo:hi], x_words_sb[:].indirect(entries(offs_sb, lo, hi)))

        w1_rest_codes = tile("w1_rest_codes", [P, 3 * P], U32, tag="x_words_sb")
        w1_rest_scales = tile("w1_rest_scales", [P, 3 * P], U8)
        quantize(w1_rest_codes[:, P:], w1_rest_scales[:, P:], w1_dealt[:, 2:].rearrange("p t m j -> p (t m j)"))
        quantize(w1_rest_codes[:, :P], w1_rest_scales[:, :P], w1_dealt[:, 1].rearrange("p m j -> p (m j)"))
        w1_tiles = stationary_tiles(w1_first_codes, w1_first_scales, 1) + stationary_tiles(w1_rest_codes, w1_rest_scales, 3)

        w3_words_sb = tile("w3_words_sb", [P, N], I32, tag="w1_raw0")
        nc.sync.dma_start(out=w3_words_sb[:], in_=as_words(w3_words))
        w2_raw = [tile("w2_raw%d" % h, [P, PLANES, H // 2], F32, tag=tag) for h, tag in enumerate(("w1_raw1", "w1_dealt"))]
        for h in range(2):
            nc.sync.dma_start(out=w2_raw[h][:], in_=w2[:, half(h)].rearrange("(p j) c -> p j c", j=PLANES))
        w3_scales_sb = tile("w3_scales_sb", [P, N], U8, tag="x_scales_sb")
        nc.gpsimd.memset(w3_scales_sb[:].bitcast(I32), 0)
        load_scale_rows(nc.sync, w3_scales_sb, w3_scales)

        y = product_planes("y", SORT_ORDER, (0, 1, 2, 3, 4), w1_tiles, picked_words, picked_scales, False)

        w3_codes = tile("w3_codes", [P, N], I32)
        nc.vector.tensor_copy(
            out=w3_codes[:].rearrange("p (t m) -> p m t", t=PLANES),
            in_=w3_words_sb[:].rearrange("p (m t) -> p m t", t=PLANES),
        )

        res_sb = tile("res_sb", [P, PLANES, S], F32, tag="x_words_sb")
        nc.sync.dma_start(out=res_sb[:], in_=res.rearrange("(p t) c -> p t c", t=PLANES))

        a = tile("a", [P, PLANES, V], F32)
        steps = [tile("steps%d" % u, [P, 2, 2, V], F32) for u in range(2)]
        for u in range(2):
            diff = tile("diff%d" % u, [P, 2, V], F32)
            for i in range(2):
                nc.vector.tensor_copy(a[:, 2 * u + i, :], y[SORT_ORDER[2 * u + i]][:].indirect(la_sb[:]))
            for i in range(2):
                looked_up = y[SORT_ORDER[2 * u + i]][:].indirect(lb_sb[:])
                nc.vector.tensor_tensor(diff[:, i, :], looked_up, a[:, 2 * u + i, :], ALU.subtract)
            drop = tile("drop%d" % u, [P, 2, V], F32)
            nc.scalar.activation(steps[u][:, 0], diff[:], ACT.Relu)
            nc.scalar.activation(drop[:], diff[:], ACT.Relu, scale=-1.0)
            nc.scalar.activation(steps[u][:, 1], drop[:], ACT.Copy, scale=-1.0)

        w2_dealt = tile("w2_dealt", [P, PLANES, P, PLANES], BF16, tag="diff0")
        for h in range(2):
            nc.scalar.copy(
                out=w2_dealt[:, :, h * P // 2 : (h + 1) * P // 2, :].rearrange("p t m j -> p m j t"),
                in_=w2_raw[h][:].rearrange("p j (m t) -> p m j t", t=PLANES),
            )
        w2_first_codes = tile("w2_first_codes", [P, 2 * P], U32)
        w2_first_scales = tile("w2_first_scales", [P, 2 * P], U8)
        quantize(w2_first_codes[:], w2_first_scales[:], w2_dealt[:, :2].rearrange("p t m j -> p (t m j)"))

        z = {t: sb.tile([P, S], F32, name="z%d" % t) for t in SORT_ORDER}
        z_bf = [tile("z_bf%d" % h, [P, HALF, PLANES], BF16) for h in range(2)]
        first, last = SORT_ORDER[0], SORT_ORDER[-1]
        for u in range(2):
            for s, places in enumerate((lb_sb, la_sb)):
                for i in range(2):
                    t = SORT_ORDER[2 * u + i]
                    nc.vector.tensor_tensor(z[t][:].indirect(places[:]), a[:, 2 * u + i, :], steps[u][:, s, i, :], ALU.add)
                    finished = s == 1
                    if finished and t == first:
                        for h in range(2):
                            twice = z[t][:, half(h)].unsqueeze(2).to_broadcast([P, HALF, 2])
                            nc.scalar.copy(out=z_bf[h][:, :, t : t + 2], in_=twice)
                    elif finished and t != last:
                        for h in range(2):
                            nc.scalar.copy(out=z_bf[h][:, :, t], in_=z[t][:, half(h)])
        quarter = S // 4
        nc.vector.tensor_copy(out=z_bf[0][:, :, last], in_=z[last][:, half(0)])
        nc.vector.tensor_copy(out=z_bf[1][:, :quarter, last], in_=z[last][:, HALF : HALF + quarter])
        nc.scalar.copy(out=z_bf[1][:, quarter:, last], in_=z[last][:, HALF + quarter :])
        z_codes = tile("z_codes", [P, S], U32)
        z_scales = tile("z_scales", [P, S], U8)
        for h in range(2):
            quantize(z_codes[:, half(h)], z_scales[:, half(h)], z_bf[h][:].rearrange("p c t -> p (c t)"))

        w2_rest_codes = tile("w2_rest_codes", [P, 2 * P], U32, tag="z_bf1")
        w2_rest_scales = tile("w2_rest_scales", [P, 2 * P], U8)
        quantize(w2_rest_codes[:], w2_rest_scales[:], w2_dealt[:, 2:].rearrange("p t m j -> p (t m j)"))
        w2_tiles = stationary_tiles(w2_first_codes, w2_first_scales, 2) + stationary_tiles(w2_rest_codes, w2_rest_scales, 2)
        hidden = product_planes("h", range(PLANES), (5, 6, 7, 0, 1), w2_tiles, z_codes, z_scales, True)

        w3_dealt_scales = tile("w3_dealt_scales", [P, N], U8, tag="diff0")
        nc.vector.tensor_copy(
            out=w3_dealt_scales[:].rearrange("p (t m) -> p m t", t=PLANES),
            in_=w3_scales_sb[:].rearrange("p (m t) -> p m t", t=PLANES),
        )
        w3_tiles = stationary_tiles(w3_codes, w3_dealt_scales, PLANES)

        stage = tile("stage", [P, 13 * UNIT], BF16)

        def staged(slot, c):
            lo, hi = SPANS[c]
            return stage[:, slot * UNIT : slot * UNIT + PLANES * (hi - lo)]

        fetched = [staged(slot, c).rearrange("p (t c) -> p t c", t=PLANES) for c, slot in enumerate((2, 0, 2))]
        z2_bf = [staged(5, 0), tile("z2_bf1", [P, PLANES * UNIT], BF16), tile("z2_bf2", [P, PLANES * UNIT], BF16)]
        z2_codes = tile("z2_codes", [P, S], U32)
        z2_scales = [tile("z2_scales%d" % c, [P, hi - lo], U8) for c, (lo, hi) in enumerate(SPANS)]
        out_codes = tile("out_codes", [P, S], U32)
        out_scales = tile("out_scales", [P, S], U8)
        out_rows = out_0.rearrange("(p t) c -> p t c", t=PLANES)
        out_words = as_words(out_1)
        result_bf = [tile("result_bf%d" % h, [P, HALF, PLANES], BF16) for h in range(2)]
        results = [tile("result%d" % c, [P, PLANES, hi - lo], F32) for c, (lo, hi) in enumerate(SPANS)]
        hidden_bf = [tile("hidden_bf%d" % h, [P, PLANES, HALF], BF16) for h in range(2)]

        def fetch(c, planes):
            lo, hi = SPANS[c]
            for t in planes:
                nc.vector.tensor_copy(fetched[c][:, t, :], hidden[t][:].indirect(entries(mate_sb, lo, hi)))

        def compete(c):
            lo, hi = SPANS[c]
            own = hidden_bf[lo // HALF][:, :, lo % HALF : lo % HALF + hi - lo]
            z2 = tile("z2_%d" % c, [P, PLANES, hi - lo], BF16)
            nc.vector.tensor_tensor(z2[:], fetched[c], own, ALU.max)
            interleave(nc.scalar.copy, z2_bf[c][:].rearrange("p (c t) -> p c t", t=PLANES), z2[:])

        def third_product(c):
            lo, hi = SPANS[c]
            quantize(z2_codes[:, lo:hi], z2_scales[c][:], z2_bf[c][:])
            accs = []
            for start in range(lo, hi, UNIT):
                acc = bank("out_acc%d" % start, 2 + start // UNIT, [P, PLANES, UNIT])
                codes = z2_codes[:, start : start + UNIT]
                scales = z2_scales[c][:, start - lo : start - lo + UNIT]
                for t in range(PLANES):
                    multiply(acc[:, t, :], w3_tiles[t], codes, scales)
                accs.append(acc)
            return accs

        def add_residual(c, accs):
            lo, hi = SPANS[c]
            for i, acc in enumerate(accs):
                start = lo + i * UNIT
                part = results[c][:, :, i * UNIT : (i + 1) * UNIT]
                nc.vector.tensor_tensor(part, acc[:], res_sb[:, :, start : start + UNIT], ALU.add)
                rounded = result_bf[start // HALF][:, start % HALF : start % HALF + UNIT, :]
                if c < len(SPANS) - 1:
                    interleave(nc.scalar.copy, rounded, part)
                else:
                    interleave(nc.scalar.copy, rounded[:, :SCALAR_ROUNDS, :], part[:, :, :SCALAR_ROUNDS])
                    interleave(nc.vector.tensor_copy, rounded[:, SCALAR_ROUNDS:, :], part[:, :, SCALAR_ROUNDS:])
            nc.sync.dma_start(out=out_rows[:, :, lo:hi], in_=results[c][:])

        def hand_on(h):
            quantize(out_codes[:, half(h)], out_scales[:, half(h)], result_bf[h][:].rearrange("p c t -> p (c t)"))
            nc.sync.dma_start(out=out_words[:, half(h)], in_=out_codes[:, half(h)].bitcast(I32))

        for h in range(2):
            for t in range(PLANES):
                nc.scalar.copy(out=hidden_bf[h][:, t, :], in_=hidden[t][:, half(h)])
        fetch(0, range(PLANES))
        fetch(1, (0, 1))
        compete(0)
        fetch(1, (2, 3))
        fetch(2, (2,))
        compete(1)
        fetch(2, (0, 1))
        accs0 = third_product(0)
        fetch(2, (3,))
        accs1 = third_product(1)
        compete(2)
        add_residual(0, accs0)
        accs2 = third_product(2)
        add_residual(1, accs1)
        hand_on(0)
        add_residual(2, accs2)
        hand_on(1)
        for q in range(4):
            queue = nc.sync if q % 2 else nc.scalar
            queue.dma_start(
                out=out_2[0, 4 * q : 4 * q + 4, :].bitcast(I32), in_=out_scales[32 * q : 32 * q + 4, :].bitcast(I32)
            )
